import numpy as np
import ml_dtypes


def mxq(x, axis, fmt="e4m3"):
    dtype, down = {"e4m3": (ml_dtypes.float8_e4m3fn, 7), "e5m2": (ml_dtypes.float8_e5m2, 14)}[fmt]
    v = np.moveaxis(np.asarray(x, np.float32).astype(ml_dtypes.bfloat16).astype(np.float64), axis, -1)
    blocks = v.reshape(v.shape[:-1] + (-1, 32))
    amax = np.abs(blocks).max(-1, keepdims=True)
    byte = np.maximum(np.where(amax > 0, np.frexp(amax)[1] - 1 + 127, 0) - down, 1)
    scale = np.exp2(byte - 127.0)
    codes = (blocks / scale).astype(np.float32).astype(dtype).astype(np.float64)
    return np.moveaxis((codes * scale).reshape(v.shape), -1, axis)


WIDE = False


def mx_kscale(k):
    if not WIDE:
        return np.ones(k)
    levels = np.array([10, -10, 5, -5, 0])
    if k % 512:
        return np.exp2(np.random.permutation(np.resize(levels, k // 32))).repeat(32)
    a = np.empty((k // 512, 16))
    for p in range(k // 512):
        a[p, :8] = np.random.permutation(np.resize(levels, 8))
        for g in range(8):
            far = levels[np.abs(levels - a[p, g]) >= 10]
            a[p, g + 8] = far[np.random.randint(len(far))]
    return np.exp2(a.ravel()).repeat(32)


def f64(x):
    return np.asarray(x).astype(np.float64)


def striped(idx):
    return np.tile(idx.reshape(-1, 16).T, (8, 1)).astype(np.uint16)


def unstriped(offs):
    return offs[:16].T.reshape(-1).astype(np.int64)


def striped8(idx):
    return np.concatenate([x.reshape(-1, 16).T for x in idx]).astype(np.uint16)


def runs(offs, k):
    lists = np.stack([offs[16 * r : 16 * r + 16].T.reshape(-1) for r in range(8)]).astype(np.int64)
    return lists[np.arange(k) % 512 // 64]


def pack_weight(w):
    k, n = w.shape
    w = f64(np.asarray(w, np.float32).astype(ml_dtypes.bfloat16)).reshape(k // 32, 32, n)
    amax = np.abs(w).max(1)
    byte = np.clip(np.where(amax > 0, np.frexp(amax)[1] - 1 + 127 - 7, 1), 1, 254)
    scaled = (w * np.exp2(127.0 - byte)[:, None, :]).reshape(k, n).astype(np.float32)
    words = np.ascontiguousarray(scaled.reshape(k // 512, 128, 4, n).transpose(0, 1, 3, 2)).astype(ml_dtypes.float8_e4m3fn).view(np.uint8)
    return words, np.ascontiguousarray(byte.astype(np.uint8).reshape(k // 512, 16, n))


def unpack_weight(words, scales):
    g, p, n, _ = words.shape
    vals = np.ascontiguousarray(words).view(ml_dtypes.float8_e4m3fn).astype(np.float64) * np.repeat(np.exp2(scales.astype(np.float64) - 127.0), 8, axis=1)[..., None]
    return vals.transpose(0, 1, 3, 2).reshape(g * 512, n)


def silu(v):
    return v / (1.0 + np.exp(-np.maximum(v, -700.0)))

def planes(y):
    n, m = y.shape
    v = y.astype(np.float32).astype(ml_dtypes.bfloat16).astype(np.float64).reshape(n // 32, 32, m)
    top = np.abs(v).max(1)
    byte = np.clip(np.where(top > 0, np.frexp(top)[1] - 1 + 127 - 7, 1), 1, 254)
    codes = (v * np.exp2(127.0 - byte)[:, None, :]).reshape(n, m).astype(np.float32).astype(ml_dtypes.float8_e4m3fn).view(np.uint8)
    words = codes.reshape(n // 512, 128, 4, m).transpose(0, 1, 3, 2)
    return np.ascontiguousarray(words), np.ascontiguousarray(byte.astype(np.uint8).reshape(n // 512, 16, m))


K, T, S, V, N, H = 512, 2048, 512, 256, 512, 512


def setup_inputs():
    n = np.random.standard_normal
    s = mx_kscale(K)[:, None]
    u = mx_kscale(S)
    packed_xT = pack_weight(n((K, T)) * s)
    packed_w1 = pack_weight(n((S, N)) / np.sqrt(S) / u[:, None])
    return {
        "x_words": packed_xT[0],
        "x_scales": packed_xT[1],
        "wa": (n((K, H)) / np.sqrt(K) / s).astype(np.float32),
        "gt": (np.random.uniform(0.5, 1.5, (S, 1)) * u[:, None]).astype(np.float32),
        "w1_words": packed_w1[0],
        "w1_scales": packed_w1[1],
        "offs": striped(np.random.permutation(T)[:S]),
        "src": striped8(np.stack([np.random.permutation(H)[:V] for _ in range(8)])),
        "dst": striped8(np.stack([np.random.permutation(H)[:V] for _ in range(8)])),
    }


def reference(x_words, x_scales, wa, gt, w1_words, w1_scales, offs, src, dst):
    xq = unpack_weight(x_words, x_scales)[:, unstriped(offs)]
    y = xq.T @ mxq(f64(wa), 0, "e4m3")
    e = silu(y[np.arange(S)[:, None], runs(src, S)] - (y[np.arange(S)[:, None], runs(dst, S)]))
    d = y.copy()
    d[np.arange(S)[:, None], runs(dst, S)] = e
    z = f64(gt) * d
    out_0 = unpack_weight(w1_words, w1_scales).T @ mxq(z, 0, "e4m3")
    return (out_0,) + planes(out_0)

@@ -1,0 +1,211 @@
+from contextlib import ExitStack
+
+import concourse.mybir as mybir
+
+F32 = mybir.dt.float32
+BF16 = mybir.dt.bfloat16
+I32 = mybir.dt.int32
+U32 = mybir.dt.uint32
+U16 = mybir.dt.uint16
+U8 = mybir.dt.uint8
+FP8X4 = mybir.dt.float8_e4m3fn_x4
+ACT = mybir.ActivationFunctionType
+ALU = mybir.AluOpType
+
+K, T, S, V, N, H = 512, 2048, 512, 256, 512, 512
+P = 128
+PACK = 4
+HALF = H // 2
+PIECE = 128
+VEC_CAST = 192
+FLOPS = 2 * K * S * H + 2 * S * N * H
+
+
+def deal_words(nc, out, in_):
+    nc.vector.tensor_copy(
+        out=out[:].rearrange("p t (c i) -> p c t i", i=4),
+        in_=in_[:].rearrange("p (c i t) -> p c t i", i=4, t=PACK),
+    )
+
+
+def deal_bytes(nc, out, in_):
+    nc.vector.tensor_copy(out=out[:], in_=in_[:].rearrange("p (m t) -> p t m", t=PACK))
+
+
+def weave(dst, src):
+    return dst.rearrange("p (c i) t -> p c t i", i=4), src.rearrange("p t (c i) -> p c t i", i=4)
+
+
+def tile_picked_featput_silu_po_kernel(tc, x_words, x_scales, wa, gt, w1_words, w1_scales, offs, src, dst, out_0, out_1, out_2):
+    nc = tc.nc
+    with ExitStack() as ctx:
+        lists = ctx.enter_context(tc.tile_pool(name="lists", bufs=1))
+        sb = ctx.enter_context(tc.tile_pool(name="sb", bufs=1))
+        ps = ctx.enter_context(tc.psum_pool(name="ps", bufs=1))
+
+        offs_t = lists.tile([P, S // 16], U16, name="offs_t")
+        src_t = lists.tile([P, V // 16], U16, name="src_t")
+        dst_t = lists.tile([P, V // 16], U16, name="dst_t")
+
+        xs_win = sb.tile([P, T], U8, name="xs_win", tag="two_kib", align_bytes=64)
+        nc.vector.memset(xs_win[:].bitcast(I32), 0)
+        nc.scalar.dma_start(out=xs_win[0:P:8, :].bitcast(I32), in_=x_scales[0].bitcast(I32))
+
+        xw_win = sb.tile([P, T], U32, name="xw_win", align_bytes=64)
+        wa_rows = wa.rearrange("(p j) c -> p j c", j=PACK)
+        wa_raw = [sb.tile([P, PACK, HALF], F32, name=f"wa_raw{h}", align_bytes=64) for h in range(2)]
+        nc.sync.dma_start(offs_t[:], offs)
+        nc.sync.dma_start(out=xw_win[:].bitcast(I32), in_=x_words[0].rearrange("p c r -> p (c r)").bitcast(I32))
+        nc.sync.dma_start(src_t[:], src)
+        nc.sync.dma_start(dst_t[:], dst)
+        for h in range(2):
+            nc.sync.dma_start(out=wa_raw[h][:], in_=wa_rows[:, :, h * HALF : (h + 1) * HALF])
+
+        w1s_raw = sb.tile([P, N], U8, name="w1s_raw", align_bytes=64)
+        nc.vector.memset(w1s_raw[:].bitcast(I32), 0)
+        nc.scalar.dma_start(out=w1s_raw[0:P:8, :].bitcast(I32), in_=w1_scales[0].bitcast(I32))
+
+        zero_in = sb.tile([P, 1], F32, name="zero_in")
+        zero = sb.tile([P, 1], F32, name="zero")
+        nc.vector.memset(zero_in[:], 0.0)
+        nc.scalar.activation(out=zero[:], in_=zero_in[:], func=ACT.Silu)
+
+        xs_got = sb.tile([P, S], U8, name="xs_got", tag="got", align_bytes=64)
+        xs_dealt = sb.tile([P, PACK, P], U8, name="xs_dealt", align_bytes=64)
+        nc.vector.tensor_copy(out=xs_got[:], in_=xs_win[:].indirect(offs_t[:]))
+        deal_bytes(nc, xs_dealt, xs_got)
+        xs_rows = xs_dealt[:].rearrange("p t m -> p (t m)").bitcast(I32)
+        for r in range(1, 4):
+            nc.scalar.dma_start(out=xs_rows[r:P:32, :], in_=xs_rows[8 * r : P : 32, :])
+
+        w1w_raw = sb.tile([P, N], U32, name="w1w_raw", tag="two_kib", align_bytes=64)
+        nc.sync.dma_start(out=w1w_raw[:].bitcast(I32), in_=w1_words[0].rearrange("p c r -> p (c r)").bitcast(I32))
+
+        xw_got = sb.tile([P, S], U32, name="xw_got", tag="got", align_bytes=64)
+        xw_dealt = sb.tile([P, PACK, P], U32, name="xw_dealt", align_bytes=64)
+        nc.vector.tensor_copy(out=xw_got[:], in_=xw_win[:].indirect(offs_t[:]))
+        deal_words(nc, xw_dealt, xw_got)
+        w1s_dealt = sb.tile([P, PACK, P], U8, name="w1s_dealt", tag="got", align_bytes=64)
+        deal_bytes(nc, w1s_dealt, w1s_raw)
+        w1s_rows = w1s_dealt[:].rearrange("p t m -> p (t m)").bitcast(I32)
+        for r in range(1, 4):
+            nc.sync.dma_start(out=w1s_rows[r:P:32, :], in_=w1s_rows[8 * r : P : 32, :])
+
+        gt_t = sb.tile([P, PACK], F32, name="gt_t", tag="w1s_raw", align_bytes=64)
+        nc.sync.dma_start(out=gt_t[:], in_=gt.rearrange("(p t) o -> p (t o)", t=PACK))
+
+        wa_bf = [sb.tile([P, HALF, PACK], BF16, name=f"wa_bf{h}", align_bytes=64) for h in range(2)]
+        wa_codes = sb.tile([P, H], U32, name="wa_codes", align_bytes=64)
+        wa_scales = sb.tile([P, H], U8, name="wa_scales", align_bytes=64)
+        o, i = weave(wa_bf[0][:], wa_raw[0][:])
+        nc.scalar.copy(out=o, in_=i)
+        o, i = weave(wa_bf[1][:, 0:VEC_CAST, :], wa_raw[1][:, :, 0:VEC_CAST])
+        nc.vector.tensor_copy(out=o, in_=i)
+        o, i = weave(wa_bf[1][:, VEC_CAST:HALF, :], wa_raw[1][:, :, VEC_CAST:HALF])
+        nc.scalar.copy(out=o, in_=i)
+        for h in range(2):
+            cols = slice(h * HALF, (h + 1) * HALF)
+            nc.vector.quantize_mx(out=wa_codes[:, cols].bitcast(FP8X4), scales=wa_scales[:, cols], in_=wa_bf[h][:].rearrange("p c t -> p (c t)"))
+
+        def first_product(out, t, cols):
+            nc.tensor.matmul_mx(
+                out=out,
+                lhsT=xw_dealt[:, t, :].bitcast(FP8X4),
+                lhsT_scale=xs_dealt[:, t, :],
+                rhs=wa_codes[:, cols].bitcast(FP8X4),
+                rhs_scale=wa_scales[:, cols],
+                start=True,
+                stop=True,
+            )
+
+        order = [2, 0, 1, 3]
+        y = [sb.tile([P, H], F32, name=f"y{t}", align_bytes=64) for t in range(PACK)]
+        left = ps.tile([P, 2, HALF], F32, name="left", tag="bank_a")
+        for s, t in enumerate(order[:2]):
+            first_product(left[:, s, :], t, slice(0, HALF))
+        for s, t in enumerate(order[:2]):
+            nc.scalar.copy(out=y[t][:, 0:HALF], in_=left[:, s, :])
+        for t in order[:2]:
+            right = ps.tile([P, HALF], F32, name=f"right{t}")
+            first_product(right[:], t, slice(HALF, H))
+            nc.scalar.copy(out=y[t][:, HALF:H], in_=right[:])
+        for t in order[2:]:
+            whole = ps.tile([P, H], F32, name=f"whole{t}")
+            first_product(whole[:], t, slice(0, H))
+            nc.scalar.copy(out=y[t][:], in_=whole[:])
+
+        b = [sb.tile([P, V], F32, name=f"b{t}", align_bytes=64) for t in range(PACK)]
+        u = [sb.tile([P, V], F32, name=f"u{t}", align_bytes=64) for t in range(PACK)]
+        e = [sb.tile([P, V], F32, name=f"e{t}", align_bytes=64) for t in range(PACK)]
+        pieces = H // PIECE
+        z_bf = [sb.tile([P, PIECE, PACK], BF16, name=f"z_bf{c}", align_bytes=64) for c in range(pieces)]
+
+        def fetch_dst(t):
+            nc.vector.tensor_copy(out=b[t][:], in_=y[t][:].indirect(dst_t[:]))
+
+        def fetch_src(t):
+            nc.vector.tensor_tensor(u[t][:], y[t][:].indirect(src_t[:]), b[t][:], ALU.subtract)
+            nc.scalar.activation(out=e[t][:], in_=u[t][:], func=ACT.Silu, bias=zero[:])
+
+        def put(t):
+            nc.vector.tensor_copy(out=y[t][:].indirect(dst_t[:]), in_=e[t][:])
+            for c in range(pieces):
+                cols = slice(c * PIECE, (c + 1) * PIECE)
+                if t == order[-1] and c < pieces // 2:
+                    nc.vector.tensor_scalar(z_bf[c][:, :, t], y[t][:, cols], gt_t[:, t : t + 1], None, ALU.mult)
+                else:
+                    nc.scalar.activation(out=z_bf[c][:, :, t], in_=y[t][:, cols], func=ACT.Copy, scale=gt_t[:, t : t + 1])
+
+        fetch_dst(order[0])
+        fetch_dst(order[1])
+        fetch_src(order[0])
+        fetch_src(order[1])
+        fetch_dst(order[2])
+        put(order[0])
+        fetch_src(order[2])
+        fetch_dst(order[3])
+        put(order[1])
+        fetch_src(order[3])
+
+        w1w_dealt = sb.tile([P, PACK, P], U32, name="w1w_dealt", align_bytes=64)
+        deal_words(nc, w1w_dealt, w1w_raw)
+
+        put(order[2])
+        put(order[3])
+
+        out_rows = out_0.rearrange("(p t) j -> p t j", t=PACK)
+        out_words = out_1[0].rearrange("p c r -> p (c r)").bitcast(I32)
+        o_codes = sb.tile([P, H], U32, name="o_codes", align_bytes=64)
+        o_scales = sb.tile([P, H], U8, name="o_scales", align_bytes=64)
+        accs = []
+        for c in range(pieces):
+            z_codes = sb.tile([P, PIECE], U32, name=f"z_codes{c}", align_bytes=64)
+            z_scales = sb.tile([P, PIECE], U8, name=f"z_scales{c}", align_bytes=64)
+            nc.vector.quantize_mx(out=z_codes[:].bitcast(FP8X4), scales=z_scales[:], in_=z_bf[c][:].rearrange("p c t -> p (c t)"))
+            acc = ps.tile([P, PACK, PIECE], F32, name=f"acc{c}", tag="bank_a" if c == pieces - 1 else f"acc{c}")
+            for t in range(PACK):
+                nc.tensor.matmul_mx(
+                    out=acc[:, t, :],
+                    lhsT=w1w_dealt[:, t, :].bitcast(FP8X4),
+                    lhsT_scale=w1s_dealt[:, t, :],
+                    rhs=z_codes[:].bitcast(FP8X4),
+                    rhs_scale=z_scales[:],
+                    start=True,
+                    stop=True,
+                )
+            accs.append(acc)
+        for c in range(pieces):
+            cols = slice(c * PIECE, (c + 1) * PIECE)
+            res = sb.tile([P, PACK, PIECE], F32, name=f"res{c}", align_bytes=64)
+            nc.scalar.copy(out=res[:], in_=accs[c][:])
+            nc.sync.dma_start(out=out_rows[:, :, cols], in_=res[:])
+            res_bf = sb.tile([P, PIECE, PACK], BF16, name=f"res_bf{c}", align_bytes=64)
+            o, i = weave(res_bf[:], res[:])
+            nc.vector.tensor_copy(out=o, in_=i)
+            nc.vector.quantize_mx(out=o_codes[:, cols].bitcast(FP8X4), scales=o_scales[:, cols], in_=res_bf[:].rearrange("p c t -> p (c t)"))
+            if c % 2 == 1:
+                pair = slice((c - 1) * PIECE, (c + 1) * PIECE)
+                nc.sync.dma_start(out=out_words[:, pair], in_=o_codes[:, pair].bitcast(I32))
+        for q in range(4):
+            queue = nc.scalar if q % 2 == 0 else nc.sync
+            queue.dma_start(out=out_2[0][4 * q : 4 * q + 4, :].bitcast(I32), in_=o_scales[32 * q : 32 * q + 4, :].bitcast(I32))

@@ -16,8 +16,10 @@ K, T, S, V, N, H = 512, 2048, 512, 256, 512, 512
 P = 128
 PACK = 4
 HALF = H // 2
-PIECE = 128
-VEC_CAST = 192
+PIECES = [256, 256]
+GROUPS = [[(0, 2), (2, 4)], [(0, 2), (2, 3), (3, 4)]]
+VEC_CAST = [168, 168]
+VEC_LAST = 160
 FLOPS = 2 * K * S * H + 2 * S * N * H
 
 
@@ -47,65 +49,61 @@ def tile_picked_featput_silu_po_kernel(tc, x_words, x_scales, wa, gt, w1_words, 
         src_t = lists.tile([P, V // 16], U16, name="src_t")
         dst_t = lists.tile([P, V // 16], U16, name="dst_t")
 
-        xs_win = sb.tile([P, T], U8, name="xs_win", tag="two_kib", align_bytes=64)
-        nc.vector.memset(xs_win[:].bitcast(I32), 0)
-        nc.scalar.dma_start(out=xs_win[0:P:8, :].bitcast(I32), in_=x_scales[0].bitcast(I32))
+        zero_in = sb.tile([P, 1], F32, name="zero_in")
+        zero = sb.tile([P, 1], F32, name="zero")
+        nc.vector.memset(zero_in[:], 0.0)
+        nc.scalar.activation(out=zero[:], in_=zero_in[:], func=ACT.Silu)
+
+        xs_win = sb.tile([P, T], U8, name="xs_win", align_bytes=64)
+        w1s_raw = sb.tile([P, N], U8, name="w1s_raw", align_bytes=64)
+        for plane in (xs_win, w1s_raw):
+            for lo, hi in ((0, 16), (32, 64), (64, P)):
+                nc.vector.memset(plane[lo:hi, :].bitcast(I32), 0)
 
         xw_win = sb.tile([P, T], U32, name="xw_win", align_bytes=64)
         wa_rows = wa.rearrange("(p j) c -> p j c", j=PACK)
         wa_raw = [sb.tile([P, PACK, HALF], F32, name=f"wa_raw{h}", align_bytes=64) for h in range(2)]
         nc.sync.dma_start(offs_t[:], offs)
+        nc.sync.dma_start(out=xs_win[16:32, :].bitcast(I32), in_=x_scales[0].bitcast(I32))
         nc.sync.dma_start(out=xw_win[:].bitcast(I32), in_=x_words[0].rearrange("p c r -> p (c r)").bitcast(I32))
         nc.sync.dma_start(src_t[:], src)
         nc.sync.dma_start(dst_t[:], dst)
         for h in range(2):
             nc.sync.dma_start(out=wa_raw[h][:], in_=wa_rows[:, :, h * HALF : (h + 1) * HALF])
-
-        w1s_raw = sb.tile([P, N], U8, name="w1s_raw", align_bytes=64)
-        nc.vector.memset(w1s_raw[:].bitcast(I32), 0)
-        nc.scalar.dma_start(out=w1s_raw[0:P:8, :].bitcast(I32), in_=w1_scales[0].bitcast(I32))
-
-        zero_in = sb.tile([P, 1], F32, name="zero_in")
-        zero = sb.tile([P, 1], F32, name="zero")
-        nc.vector.memset(zero_in[:], 0.0)
-        nc.scalar.activation(out=zero[:], in_=zero_in[:], func=ACT.Silu)
+        gt_t = sb.tile([P, PACK], F32, name="gt_t", align_bytes=64)
+        nc.sync.dma_start(out=gt_t[:], in_=gt.rearrange("(p t) o -> p (t o)", t=PACK))
+        nc.scalar.dma_start(out=w1s_raw[16:32, :].bitcast(I32), in_=w1_scales[0].bitcast(I32))
 
         xs_got = sb.tile([P, S], U8, name="xs_got", tag="got", align_bytes=64)
         xs_dealt = sb.tile([P, PACK, P], U8, name="xs_dealt", align_bytes=64)
         nc.vector.tensor_copy(out=xs_got[:], in_=xs_win[:].indirect(offs_t[:]))
         deal_bytes(nc, xs_dealt, xs_got)
         xs_rows = xs_dealt[:].rearrange("p t m -> p (t m)").bitcast(I32)
-        for r in range(1, 4):
-            nc.scalar.dma_start(out=xs_rows[r:P:32, :], in_=xs_rows[8 * r : P : 32, :])
+        for q in range(4):
+            nc.sync.dma_start(out=xs_rows[32 * q : 32 * q + 4, :], in_=xs_rows[16 + 4 * q : 20 + 4 * q, :])
 
-        w1w_raw = sb.tile([P, N], U32, name="w1w_raw", tag="two_kib", align_bytes=64)
+        w1w_raw = sb.tile([P, N], U32, name="w1w_raw", tag="got", align_bytes=64)
         nc.sync.dma_start(out=w1w_raw[:].bitcast(I32), in_=w1_words[0].rearrange("p c r -> p (c r)").bitcast(I32))
 
-        xw_got = sb.tile([P, S], U32, name="xw_got", tag="got", align_bytes=64)
-        xw_dealt = sb.tile([P, PACK, P], U32, name="xw_dealt", align_bytes=64)
-        nc.vector.tensor_copy(out=xw_got[:], in_=xw_win[:].indirect(offs_t[:]))
-        deal_words(nc, xw_dealt, xw_got)
-        w1s_dealt = sb.tile([P, PACK, P], U8, name="w1s_dealt", tag="got", align_bytes=64)
+        w1s_dealt = sb.tile([P, PACK, P], U8, name="w1s_dealt", tag="xs_win", align_bytes=64)
         deal_bytes(nc, w1s_dealt, w1s_raw)
         w1s_rows = w1s_dealt[:].rearrange("p t m -> p (t m)").bitcast(I32)
-        for r in range(1, 4):
-            nc.sync.dma_start(out=w1s_rows[r:P:32, :], in_=w1s_rows[8 * r : P : 32, :])
+        for q in range(4):
+            nc.sync.dma_start(out=w1s_rows[32 * q : 32 * q + 4, :], in_=w1s_rows[16 + 4 * q : 20 + 4 * q, :])
 
-        gt_t = sb.tile([P, PACK], F32, name="gt_t", tag="w1s_raw", align_bytes=64)
-        nc.sync.dma_start(out=gt_t[:], in_=gt.rearrange("(p t) o -> p (t o)", t=PACK))
+        xw_dealt = sb.tile([P, PACK, P], U32, name="xw_dealt", align_bytes=64)
+        nc.vector.tensor_copy(out=xw_dealt[:].rearrange("p t m -> p m t"), in_=xw_win[:].indirect(offs_t[:]))
 
-        wa_bf = [sb.tile([P, HALF, PACK], BF16, name=f"wa_bf{h}", align_bytes=64) for h in range(2)]
         wa_codes = sb.tile([P, H], U32, name="wa_codes", align_bytes=64)
         wa_scales = sb.tile([P, H], U8, name="wa_scales", align_bytes=64)
-        o, i = weave(wa_bf[0][:], wa_raw[0][:])
-        nc.scalar.copy(out=o, in_=i)
-        o, i = weave(wa_bf[1][:, 0:VEC_CAST, :], wa_raw[1][:, :, 0:VEC_CAST])
-        nc.vector.tensor_copy(out=o, in_=i)
-        o, i = weave(wa_bf[1][:, VEC_CAST:HALF, :], wa_raw[1][:, :, VEC_CAST:HALF])
-        nc.scalar.copy(out=o, in_=i)
         for h in range(2):
+            wa_bf = sb.tile([P, HALF, PACK], BF16, name=f"wa_bf{h}", tag="xw_win", align_bytes=64)
+            o, i = weave(wa_bf[:, 0 : VEC_CAST[h], :], wa_raw[h][:, :, 0 : VEC_CAST[h]])
+            nc.vector.tensor_copy(out=o, in_=i)
+            o, i = weave(wa_bf[:, VEC_CAST[h] : HALF, :], wa_raw[h][:, :, VEC_CAST[h] : HALF])
+            nc.scalar.copy(out=o, in_=i)
             cols = slice(h * HALF, (h + 1) * HALF)
-            nc.vector.quantize_mx(out=wa_codes[:, cols].bitcast(FP8X4), scales=wa_scales[:, cols], in_=wa_bf[h][:].rearrange("p c t -> p (c t)"))
+            nc.vector.quantize_mx(out=wa_codes[:, cols].bitcast(FP8X4), scales=wa_scales[:, cols], in_=wa_bf[:].rearrange("p c t -> p (c t)"))
 
         def first_product(out, t, cols):
             nc.tensor.matmul_mx(
@@ -120,42 +118,43 @@ def tile_picked_featput_silu_po_kernel(tc, x_words, x_scales, wa, gt, w1_words, 
 
         order = [2, 0, 1, 3]
         y = [sb.tile([P, H], F32, name=f"y{t}", align_bytes=64) for t in range(PACK)]
-        left = ps.tile([P, 2, HALF], F32, name="left", tag="bank_a")
-        for s, t in enumerate(order[:2]):
-            first_product(left[:, s, :], t, slice(0, HALF))
-        for s, t in enumerate(order[:2]):
-            nc.scalar.copy(out=y[t][:, 0:HALF], in_=left[:, s, :])
-        for t in order[:2]:
-            right = ps.tile([P, HALF], F32, name=f"right{t}")
-            first_product(right[:], t, slice(HALF, H))
-            nc.scalar.copy(out=y[t][:, HALF:H], in_=right[:])
+        for h in range(2):
+            cols = slice(h * HALF, (h + 1) * HALF)
+            for s, t in enumerate(order[:2]):
+                part = ps.tile([P, HALF], F32, name=f"part{t}_{h}", tag=f"bank{2 * h + s}")
+                first_product(part[:], t, cols)
+                nc.scalar.copy(out=y[t][:, cols], in_=part[:])
         for t in order[2:]:
-            whole = ps.tile([P, H], F32, name=f"whole{t}")
+            whole = ps.tile([P, H], F32, name=f"whole{t}", tag=f"bank{2 + order.index(t)}")
             first_product(whole[:], t, slice(0, H))
             nc.scalar.copy(out=y[t][:], in_=whole[:])
 
-        b = [sb.tile([P, V], F32, name=f"b{t}", align_bytes=64) for t in range(PACK)]
-        u = [sb.tile([P, V], F32, name=f"u{t}", align_bytes=64) for t in range(PACK)]
-        e = [sb.tile([P, V], F32, name=f"e{t}", align_bytes=64) for t in range(PACK)]
-        pieces = H // PIECE
-        z_bf = [sb.tile([P, PIECE, PACK], BF16, name=f"z_bf{c}", align_bytes=64) for c in range(pieces)]
+        w1w_dealt = sb.tile([P, PACK, P], U32, name="w1w_dealt", tag="xw_win", align_bytes=64)
+        b = {}
+        e = {}
+        starts = [sum(PIECES[:c]) for c in range(len(PIECES))]
+        z_bf = [sb.tile([P, w, PACK], BF16, name=f"z_bf{c}", align_bytes=64) for c, w in enumerate(PIECES)]
 
         def fetch_dst(t):
+            b[t] = sb.tile([P, V], F32, name=f"b{t}", tag=f"e{order[0]}" if t == order[3] else f"b{t}", align_bytes=64)
             nc.vector.tensor_copy(out=b[t][:], in_=y[t][:].indirect(dst_t[:]))
 
         def fetch_src(t):
-            nc.vector.tensor_tensor(u[t][:], y[t][:].indirect(src_t[:]), b[t][:], ALU.subtract)
-            nc.scalar.activation(out=e[t][:], in_=u[t][:], func=ACT.Silu, bias=zero[:])
+            u = sb.tile([P, V], F32, name=f"u{t}", tag=f"u{order.index(t) % 2}", align_bytes=64)
+            nc.vector.tensor_tensor(u[:], y[t][:].indirect(src_t[:]), b[t][:], ALU.subtract)
+            e[t] = sb.tile([P, V], F32, name=f"e{t}", align_bytes=64)
+            nc.scalar.activation(out=e[t][:], in_=u[:], func=ACT.Silu, bias=zero[:])
 
         def put(t):
             nc.vector.tensor_copy(out=y[t][:].indirect(dst_t[:]), in_=e[t][:])
-            for c in range(pieces):
-                cols = slice(c * PIECE, (c + 1) * PIECE)
-                if t == order[-1] and c < pieces // 2:
+            for c, w in enumerate(PIECES):
+                cols = slice(starts[c], starts[c] + w)
+                if t == order[-1] and c == 0:
                     nc.vector.tensor_scalar(z_bf[c][:, :, t], y[t][:, cols], gt_t[:, t : t + 1], None, ALU.mult)
                 else:
                     nc.scalar.activation(out=z_bf[c][:, :, t], in_=y[t][:, cols], func=ACT.Copy, scale=gt_t[:, t : t + 1])
 
+        deal_words(nc, w1w_dealt, w1w_raw)
         fetch_dst(order[0])
         fetch_dst(order[1])
         fetch_src(order[0])
@@ -166,10 +165,6 @@ def tile_picked_featput_silu_po_kernel(tc, x_words, x_scales, wa, gt, w1_words, 
         fetch_dst(order[3])
         put(order[1])
         fetch_src(order[3])
-
-        w1w_dealt = sb.tile([P, PACK, P], U32, name="w1w_dealt", align_bytes=64)
-        deal_words(nc, w1w_dealt, w1w_raw)
-
         put(order[2])
         put(order[3])
 
@@ -177,35 +172,45 @@ def tile_picked_featput_silu_po_kernel(tc, x_words, x_scales, wa, gt, w1_words, 
         out_words = out_1[0].rearrange("p c r -> p (c r)").bitcast(I32)
         o_codes = sb.tile([P, H], U32, name="o_codes", align_bytes=64)
         o_scales = sb.tile([P, H], U8, name="o_scales", align_bytes=64)
-        accs = []
-        for c in range(pieces):
-            z_codes = sb.tile([P, PIECE], U32, name=f"z_codes{c}", align_bytes=64)
-            z_scales = sb.tile([P, PIECE], U8, name=f"z_scales{c}", align_bytes=64)
+        free_banks = [f"bank{k}" for k in range(5)]
+        banks = {}
+        for c, w in enumerate(PIECES):
+            z_codes = sb.tile([P, w], U32, name=f"z_codes{c}", align_bytes=64)
+            z_scales = sb.tile([P, w], U8, name=f"z_scales{c}", align_bytes=64)
             nc.vector.quantize_mx(out=z_codes[:].bitcast(FP8X4), scales=z_scales[:], in_=z_bf[c][:].rearrange("p c t -> p (c t)"))
-            acc = ps.tile([P, PACK, PIECE], F32, name=f"acc{c}", tag="bank_a" if c == pieces - 1 else f"acc{c}")
-            for t in range(PACK):
-                nc.tensor.matmul_mx(
-                    out=acc[:, t, :],
-                    lhsT=w1w_dealt[:, t, :].bitcast(FP8X4),
-                    lhsT_scale=w1s_dealt[:, t, :],
-                    rhs=z_codes[:].bitcast(FP8X4),
-                    rhs_scale=z_scales[:],
-                    start=True,
-                    stop=True,
-                )
-            accs.append(acc)
-        for c in range(pieces):
-            cols = slice(c * PIECE, (c + 1) * PIECE)
-            res = sb.tile([P, PACK, PIECE], F32, name=f"res{c}", align_bytes=64)
-            nc.scalar.copy(out=res[:], in_=accs[c][:])
-            nc.sync.dma_start(out=out_rows[:, :, cols], in_=res[:])
-            res_bf = sb.tile([P, PIECE, PACK], BF16, name=f"res_bf{c}", align_bytes=64)
-            o, i = weave(res_bf[:], res[:])
+            for t0, t1 in GROUPS[c]:
+                acc = ps.tile([P, t1 - t0, w], F32, name=f"acc{c}_{t0}", tag=free_banks.pop())
+                for t in range(t0, t1):
+                    nc.tensor.matmul_mx(
+                        out=acc[:, t - t0, :],
+                        lhsT=w1w_dealt[:, t, :].bitcast(FP8X4),
+                        lhsT_scale=w1s_dealt[:, t, :],
+                        rhs=z_codes[:].bitcast(FP8X4),
+                        rhs_scale=z_scales[:],
+                        start=True,
+                        stop=True,
+                    )
+                banks[(c, t0)] = acc
+        stored = 0
+        for c, w in enumerate(PIECES):
+            cols = slice(starts[c], starts[c] + w)
+            res = sb.tile([P, PACK, w], F32, name=f"res{c}", align_bytes=64)
+            res_bf = sb.tile([P, w, PACK], BF16, name=f"res_bf{c}", align_bytes=64)
+            for t0, t1 in GROUPS[c]:
+                nc.scalar.copy(out=res[:, t0:t1, :], in_=banks[(c, t0)][:])
+                if t1 % 2 == 0:
+                    nc.sync.dma_start(out=out_rows[:, t1 - 2 : t1, cols], in_=res[:, t1 - 2 : t1, :])
+            split = w if c == 0 else VEC_LAST
+            o, i = weave(res_bf[:, 0:split, :], res[:, :, 0:split])
             nc.vector.tensor_copy(out=o, in_=i)
+            if split < w:
+                o, i = weave(res_bf[:, split:w, :], res[:, :, split:w])
+                nc.scalar.copy(out=o, in_=i)
             nc.vector.quantize_mx(out=o_codes[:, cols].bitcast(FP8X4), scales=o_scales[:, cols], in_=res_bf[:].rearrange("p c t -> p (c t)"))
-            if c % 2 == 1:
-                pair = slice((c - 1) * PIECE, (c + 1) * PIECE)
-                nc.sync.dma_start(out=out_words[:, pair], in_=o_codes[:, pair].bitcast(I32))
+            if c >= len(PIECES) - 2:
+                run = slice(stored, cols.stop)
+                (nc.scalar if cols.stop == H else nc.sync).dma_start(out=out_words[:, run], in_=o_codes[:, run].bitcast(I32))
+                stored = cols.stop
         for q in range(4):
-            queue = nc.scalar if q % 2 == 0 else nc.sync
+            queue = nc.scalar if q == 3 else nc.sync
             queue.dma_start(out=out_2[0][4 * q : 4 * q + 4, :].bitcast(I32), in_=o_scales[32 * q : 32 * q + 4, :].bitcast(I32))

@@ -18,8 +18,7 @@ PACK = 4
 HALF = H // 2
 PIECES = [256, 256]
 GROUPS = [[(0, 2), (2, 4)], [(0, 2), (2, 3), (3, 4)]]
-VEC_CAST = [168, 168]
-VEC_LAST = 160
+VEC_SHARE = 160
 FLOPS = 2 * K * S * H + 2 * S * N * H
 
 
@@ -61,18 +60,16 @@ def tile_picked_featput_silu_po_kernel(tc, x_words, x_scales, wa, gt, w1_words, 
                 nc.vector.memset(plane[lo:hi, :].bitcast(I32), 0)
 
         xw_win = sb.tile([P, T], U32, name="xw_win", align_bytes=64)
-        wa_rows = wa.rearrange("(p j) c -> p j c", j=PACK)
-        wa_raw = [sb.tile([P, PACK, HALF], F32, name=f"wa_raw{h}", align_bytes=64) for h in range(2)]
+        wa_raw = sb.tile([P, PACK, H], F32, name="wa_raw", align_bytes=64)
+        gt_t = sb.tile([P, PACK], F32, name="gt_t", align_bytes=64)
         nc.sync.dma_start(offs_t[:], offs)
+        nc.scalar.dma_start(out=w1s_raw[16:32, :].bitcast(I32), in_=w1_scales[0].bitcast(I32))
+        nc.scalar.dma_start(out=gt_t[:], in_=gt.rearrange("(p t) o -> p (t o)", t=PACK))
         nc.sync.dma_start(out=xs_win[16:32, :].bitcast(I32), in_=x_scales[0].bitcast(I32))
         nc.sync.dma_start(out=xw_win[:].bitcast(I32), in_=x_words[0].rearrange("p c r -> p (c r)").bitcast(I32))
+        nc.sync.dma_start(out=wa_raw[:], in_=wa.rearrange("(p j) c -> p j c", j=PACK))
         nc.sync.dma_start(src_t[:], src)
         nc.sync.dma_start(dst_t[:], dst)
-        for h in range(2):
-            nc.sync.dma_start(out=wa_raw[h][:], in_=wa_rows[:, :, h * HALF : (h + 1) * HALF])
-        gt_t = sb.tile([P, PACK], F32, name="gt_t", align_bytes=64)
-        nc.sync.dma_start(out=gt_t[:], in_=gt.rearrange("(p t) o -> p (t o)", t=PACK))
-        nc.scalar.dma_start(out=w1s_raw[16:32, :].bitcast(I32), in_=w1_scales[0].bitcast(I32))
 
         xs_got = sb.tile([P, S], U8, name="xs_got", tag="got", align_bytes=64)
         xs_dealt = sb.tile([P, PACK, P], U8, name="xs_dealt", align_bytes=64)
@@ -80,7 +77,7 @@ def tile_picked_featput_silu_po_kernel(tc, x_words, x_scales, wa, gt, w1_words, 
         deal_bytes(nc, xs_dealt, xs_got)
         xs_rows = xs_dealt[:].rearrange("p t m -> p (t m)").bitcast(I32)
         for q in range(4):
-            nc.sync.dma_start(out=xs_rows[32 * q : 32 * q + 4, :], in_=xs_rows[16 + 4 * q : 20 + 4 * q, :])
+            nc.scalar.dma_start(out=xs_rows[32 * q : 32 * q + 4, :], in_=xs_rows[16 + 4 * q : 20 + 4 * q, :])
 
         w1w_raw = sb.tile([P, N], U32, name="w1w_raw", tag="got", align_bytes=64)
         nc.sync.dma_start(out=w1w_raw[:].bitcast(I32), in_=w1_words[0].rearrange("p c r -> p (c r)").bitcast(I32))
@@ -92,18 +89,22 @@ def tile_picked_featput_silu_po_kernel(tc, x_words, x_scales, wa, gt, w1_words, 
             nc.sync.dma_start(out=w1s_rows[32 * q : 32 * q + 4, :], in_=w1s_rows[16 + 4 * q : 20 + 4 * q, :])
 
         xw_dealt = sb.tile([P, PACK, P], U32, name="xw_dealt", align_bytes=64)
-        nc.vector.tensor_copy(out=xw_dealt[:].rearrange("p t m -> p m t"), in_=xw_win[:].indirect(offs_t[:]))
+        xw_got = sb.tile([P, S], U32, name="xw_got", align_bytes=64)
+        nc.vector.tensor_copy(out=xw_got[:], in_=xw_win[:].indirect(offs_t[:]))
+        deal_words(nc, xw_dealt, xw_got)
 
-        wa_codes = sb.tile([P, H], U32, name="wa_codes", align_bytes=64)
+        wa_codes = sb.tile([P, H], U32, name="wa_codes", tag="xw_got", align_bytes=64)
         wa_scales = sb.tile([P, H], U8, name="wa_scales", align_bytes=64)
+        wa_bf = [sb.tile([P, HALF, PACK], BF16, name=f"wa_bf{h}", align_bytes=64) for h in range(2)]
         for h in range(2):
-            wa_bf = sb.tile([P, HALF, PACK], BF16, name=f"wa_bf{h}", tag="xw_win", align_bytes=64)
-            o, i = weave(wa_bf[:, 0 : VEC_CAST[h], :], wa_raw[h][:, :, 0 : VEC_CAST[h]])
+            c0 = h * HALF
+            o, i = weave(wa_bf[h][:, 0:VEC_SHARE, :], wa_raw[:, :, c0 : c0 + VEC_SHARE])
             nc.vector.tensor_copy(out=o, in_=i)
-            o, i = weave(wa_bf[:, VEC_CAST[h] : HALF, :], wa_raw[h][:, :, VEC_CAST[h] : HALF])
+            o, i = weave(wa_bf[h][:, VEC_SHARE:HALF, :], wa_raw[:, :, c0 + VEC_SHARE : c0 + HALF])
             nc.scalar.copy(out=o, in_=i)
+        for h in range(2):
             cols = slice(h * HALF, (h + 1) * HALF)
-            nc.vector.quantize_mx(out=wa_codes[:, cols].bitcast(FP8X4), scales=wa_scales[:, cols], in_=wa_bf[:].rearrange("p c t -> p (c t)"))
+            nc.vector.quantize_mx(out=wa_codes[:, cols].bitcast(FP8X4), scales=wa_scales[:, cols], in_=wa_bf[h][:].rearrange("p c t -> p (c t)"))
 
         def first_product(out, t, cols):
             nc.tensor.matmul_mx(
@@ -118,18 +119,20 @@ def tile_picked_featput_silu_po_kernel(tc, x_words, x_scales, wa, gt, w1_words, 
 
         order = [2, 0, 1, 3]
         y = [sb.tile([P, H], F32, name=f"y{t}", align_bytes=64) for t in range(PACK)]
-        for h in range(2):
-            cols = slice(h * HALF, (h + 1) * HALF)
-            for s, t in enumerate(order[:2]):
-                part = ps.tile([P, HALF], F32, name=f"part{t}_{h}", tag=f"bank{2 * h + s}")
-                first_product(part[:], t, cols)
-                nc.scalar.copy(out=y[t][:, cols], in_=part[:])
-        for t in order[2:]:
-            whole = ps.tile([P, H], F32, name=f"whole{t}", tag=f"bank{2 + order.index(t)}")
-            first_product(whole[:], t, slice(0, H))
-            nc.scalar.copy(out=y[t][:], in_=whole[:])
+        left, right, whole = slice(0, HALF), slice(HALF, H), slice(0, H)
+        for t, cols, bank in (
+            (order[0], left, 0),
+            (order[1], left, 1),
+            (order[0], right, 2),
+            (order[1], right, 3),
+            (order[2], whole, 4),
+            (order[3], whole, 5),
+        ):
+            part = ps.tile([P, cols.stop - cols.start], F32, name=f"part{t}_{cols.start}", tag=f"bank{bank}")
+            first_product(part[:], t, cols)
+            nc.scalar.copy(out=y[t][:, cols], in_=part[:])
 
-        w1w_dealt = sb.tile([P, PACK, P], U32, name="w1w_dealt", tag="xw_win", align_bytes=64)
+        w1w_dealt = sb.tile([P, PACK, P], U32, name="w1w_dealt", tag="wa_bf1", align_bytes=64)
         b = {}
         e = {}
         starts = [sum(PIECES[:c]) for c in range(len(PIECES))]
@@ -149,7 +152,7 @@ def tile_picked_featput_silu_po_kernel(tc, x_words, x_scales, wa, gt, w1_words, 
             nc.vector.tensor_copy(out=y[t][:].indirect(dst_t[:]), in_=e[t][:])
             for c, w in enumerate(PIECES):
                 cols = slice(starts[c], starts[c] + w)
-                if t == order[-1] and c == 0:
+                if t == order[-1] and starts[c] < HALF:
                     nc.vector.tensor_scalar(z_bf[c][:, :, t], y[t][:, cols], gt_t[:, t : t + 1], None, ALU.mult)
                 else:
                     nc.scalar.activation(out=z_bf[c][:, :, t], in_=y[t][:, cols], func=ACT.Copy, scale=gt_t[:, t : t + 1])
@@ -199,8 +202,9 @@ def tile_picked_featput_silu_po_kernel(tc, x_words, x_scales, wa, gt, w1_words, 
             for t0, t1 in GROUPS[c]:
                 nc.scalar.copy(out=res[:, t0:t1, :], in_=banks[(c, t0)][:])
                 if t1 % 2 == 0:
-                    nc.sync.dma_start(out=out_rows[:, t1 - 2 : t1, cols], in_=res[:, t1 - 2 : t1, :])
-            split = w if c == 0 else VEC_LAST
+                    rows = slice(t0 - t0 % 2, t1)
+                    nc.sync.dma_start(out=out_rows[:, rows, cols], in_=res[:, rows, :])
+            split = VEC_SHARE if cols.stop == H else w
             o, i = weave(res_bf[:, 0:split, :], res[:, :, 0:split])
             nc.vector.tensor_copy(out=o, in_=i)
             if split < w:

@@ -15,10 +15,12 @@ ALU = mybir.AluOpType
 K, T, S, V, N, H = 512, 2048, 512, 256, 512, 512
 P = 128
 PACK = 4
+QUADS = 4
 HALF = H // 2
-PIECES = [256, 256]
-GROUPS = [[(0, 2), (2, 4)], [(0, 2), (2, 3), (3, 4)]]
+PIECES = [slice(0, P), slice(P, HALF), slice(HALF, H)]
+STORES = [[slice(0, 1), slice(1, 2), slice(2, 4)], [slice(0, 2), slice(2, 4)]]
 VEC_SHARE = 160
+ORDER = [2, 0, 1, 3]
 FLOPS = 2 * K * S * H + 2 * S * N * H
 
 
@@ -33,12 +35,43 @@ def deal_bytes(nc, out, in_):
     nc.vector.tensor_copy(out=out[:], in_=in_[:].rearrange("p (m t) -> p t m", t=PACK))
 
 
-def weave(dst, src):
-    return dst.rearrange("p (c i) t -> p c t i", i=4), src.rearrange("p t (c i) -> p c t i", i=4)
+def place_scale_rows(queue, plane):
+    rows = plane[:].rearrange("p t m -> p (t m)").bitcast(I32)
+    for q in range(QUADS):
+        queue.dma_start(out=rows[32 * q : 32 * q + 4, :], in_=rows[16 + 4 * q : 20 + 4 * q, :])
 
 
-def tile_picked_featput_silu_po_kernel(tc, x_words, x_scales, wa, gt, w1_words, w1_scales, offs, src, dst, out_0, out_1, out_2):
+def interleave(nc, out, in_, vec_cols):
+    width = out.shape[1]
+    for copy, cols in ((nc.vector.tensor_copy, slice(0, vec_cols)), (nc.scalar.copy, slice(vec_cols, width))):
+        if cols.start < cols.stop:
+            copy(
+                out=out[:, cols, :].rearrange("p (c i) t -> p c t i", i=4),
+                in_=in_[:, :, cols].rearrange("p t (c i) -> p c t i", i=4),
+            )
+
+
+def quantize(nc, codes, scales, grouped):
+    nc.vector.quantize_mx(out=codes.bitcast(FP8X4), scales=scales, in_=grouped[:].rearrange("p c t -> p (c t)"))
+
+
+def product(nc, out, lhs_words, lhs_scales, rhs_codes, rhs_scales):
+    nc.tensor.matmul_mx(
+        out=out,
+        lhsT=lhs_words.bitcast(FP8X4),
+        lhsT_scale=lhs_scales,
+        rhs=rhs_codes.bitcast(FP8X4),
+        rhs_scale=rhs_scales,
+        start=True,
+        stop=True,
+    )
+
+
+def tile_picked_featput_silu_po_kernel(
+    tc, x_words, x_scales, wa, gt, w1_words, w1_scales, offs, src, dst, out_0, out_1, out_2
+):
     nc = tc.nc
+    halves = [slice(0, HALF), slice(HALF, H)]
     with ExitStack() as ctx:
         lists = ctx.enter_context(tc.tile_pool(name="lists", bufs=1))
         sb = ctx.enter_context(tc.tile_pool(name="sb", bufs=1))
@@ -71,22 +104,17 @@ def tile_picked_featput_silu_po_kernel(tc, x_words, x_scales, wa, gt, w1_words, 
         nc.sync.dma_start(src_t[:], src)
         nc.sync.dma_start(dst_t[:], dst)
 
-        xs_got = sb.tile([P, S], U8, name="xs_got", tag="got", align_bytes=64)
+        xs_got = sb.tile([P, S], U8, name="xs_got", align_bytes=64)
         xs_dealt = sb.tile([P, PACK, P], U8, name="xs_dealt", align_bytes=64)
         nc.vector.tensor_copy(out=xs_got[:], in_=xs_win[:].indirect(offs_t[:]))
         deal_bytes(nc, xs_dealt, xs_got)
-        xs_rows = xs_dealt[:].rearrange("p t m -> p (t m)").bitcast(I32)
-        for q in range(4):
-            nc.scalar.dma_start(out=xs_rows[32 * q : 32 * q + 4, :], in_=xs_rows[16 + 4 * q : 20 + 4 * q, :])
+        place_scale_rows(nc.scalar, xs_dealt)
 
-        w1w_raw = sb.tile([P, N], U32, name="w1w_raw", tag="got", align_bytes=64)
+        w1w_raw = sb.tile([P, N], U32, name="w1w_raw", tag="xs_got", align_bytes=64)
         nc.sync.dma_start(out=w1w_raw[:].bitcast(I32), in_=w1_words[0].rearrange("p c r -> p (c r)").bitcast(I32))
-
         w1s_dealt = sb.tile([P, PACK, P], U8, name="w1s_dealt", tag="xs_win", align_bytes=64)
         deal_bytes(nc, w1s_dealt, w1s_raw)
-        w1s_rows = w1s_dealt[:].rearrange("p t m -> p (t m)").bitcast(I32)
-        for q in range(4):
-            nc.sync.dma_start(out=w1s_rows[32 * q : 32 * q + 4, :], in_=w1s_rows[16 + 4 * q : 20 + 4 * q, :])
+        place_scale_rows(nc.sync, w1s_dealt)
 
         xw_dealt = sb.tile([P, PACK, P], U32, name="xw_dealt", align_bytes=64)
         xw_got = sb.tile([P, S], U32, name="xw_got", align_bytes=64)
@@ -96,125 +124,92 @@ def tile_picked_featput_silu_po_kernel(tc, x_words, x_scales, wa, gt, w1_words, 
         wa_codes = sb.tile([P, H], U32, name="wa_codes", tag="xw_got", align_bytes=64)
         wa_scales = sb.tile([P, H], U8, name="wa_scales", align_bytes=64)
         wa_bf = [sb.tile([P, HALF, PACK], BF16, name=f"wa_bf{h}", align_bytes=64) for h in range(2)]
-        for h in range(2):
-            c0 = h * HALF
-            o, i = weave(wa_bf[h][:, 0:VEC_SHARE, :], wa_raw[:, :, c0 : c0 + VEC_SHARE])
-            nc.vector.tensor_copy(out=o, in_=i)
-            o, i = weave(wa_bf[h][:, VEC_SHARE:HALF, :], wa_raw[:, :, c0 + VEC_SHARE : c0 + HALF])
-            nc.scalar.copy(out=o, in_=i)
-        for h in range(2):
-            cols = slice(h * HALF, (h + 1) * HALF)
-            nc.vector.quantize_mx(out=wa_codes[:, cols].bitcast(FP8X4), scales=wa_scales[:, cols], in_=wa_bf[h][:].rearrange("p c t -> p (c t)"))
+        for h, cols in enumerate(halves):
+            interleave(nc, wa_bf[h][:], wa_raw[:, :, cols], VEC_SHARE)
+        for h, cols in enumerate(halves):
+            quantize(nc, wa_codes[:, cols], wa_scales[:, cols], wa_bf[h])
 
-        def first_product(out, t, cols):
-            nc.tensor.matmul_mx(
-                out=out,
-                lhsT=xw_dealt[:, t, :].bitcast(FP8X4),
-                lhsT_scale=xs_dealt[:, t, :],
-                rhs=wa_codes[:, cols].bitcast(FP8X4),
-                rhs_scale=wa_scales[:, cols],
-                start=True,
-                stop=True,
-            )
-
-        order = [2, 0, 1, 3]
         y = [sb.tile([P, H], F32, name=f"y{t}", align_bytes=64) for t in range(PACK)]
-        left, right, whole = slice(0, HALF), slice(HALF, H), slice(0, H)
-        for t, cols, bank in (
-            (order[0], left, 0),
-            (order[1], left, 1),
-            (order[0], right, 2),
-            (order[1], right, 3),
-            (order[2], whole, 4),
-            (order[3], whole, 5),
-        ):
-            part = ps.tile([P, cols.stop - cols.start], F32, name=f"part{t}_{cols.start}", tag=f"bank{bank}")
-            first_product(part[:], t, cols)
+        parts = [(t, cols) for cols in halves for t in ORDER[:2]] + [(t, slice(0, H)) for t in ORDER[2:]]
+        for bank, (t, cols) in enumerate(parts):
+            part = ps.tile([P, cols.stop - cols.start], F32, name=f"part{bank}", tag=f"bank{bank}")
+            product(nc, part[:], xw_dealt[:, t, :], xs_dealt[:, t, :], wa_codes[:, cols], wa_scales[:, cols])
             nc.scalar.copy(out=y[t][:, cols], in_=part[:])
 
         w1w_dealt = sb.tile([P, PACK, P], U32, name="w1w_dealt", tag="wa_bf1", align_bytes=64)
-        b = {}
-        e = {}
-        starts = [sum(PIECES[:c]) for c in range(len(PIECES))]
-        z_bf = [sb.tile([P, w, PACK], BF16, name=f"z_bf{c}", align_bytes=64) for c, w in enumerate(PIECES)]
+        z_bf = [
+            sb.tile([P, cols.stop - cols.start, PACK], BF16, name=f"z_bf{c}", align_bytes=64)
+            for c, cols in enumerate(PIECES)
+        ]
+        old = {}
+        new = {}
 
-        def fetch_dst(t):
-            b[t] = sb.tile([P, V], F32, name=f"b{t}", tag=f"e{order[0]}" if t == order[3] else f"b{t}", align_bytes=64)
-            nc.vector.tensor_copy(out=b[t][:], in_=y[t][:].indirect(dst_t[:]))
+        def fetch_old(t):
+            tag = f"new{ORDER[0]}" if t == ORDER[-1] else f"old{t}"
+            old[t] = sb.tile([P, V], F32, name=f"old{t}", tag=tag, align_bytes=64)
+            nc.vector.tensor_copy(out=old[t][:], in_=y[t][:].indirect(dst_t[:]))
 
-        def fetch_src(t):
-            u = sb.tile([P, V], F32, name=f"u{t}", tag=f"u{order.index(t) % 2}", align_bytes=64)
-            nc.vector.tensor_tensor(u[:], y[t][:].indirect(src_t[:]), b[t][:], ALU.subtract)
-            e[t] = sb.tile([P, V], F32, name=f"e{t}", align_bytes=64)
-            nc.scalar.activation(out=e[t][:], in_=u[:], func=ACT.Silu, bias=zero[:])
+        def make_new(t):
+            diff = sb.tile([P, V], F32, name=f"diff{t}", tag=f"diff{ORDER.index(t) % 2}", align_bytes=64)
+            nc.vector.tensor_tensor(diff[:], y[t][:].indirect(src_t[:]), old[t][:], ALU.subtract)
+            new[t] = sb.tile([P, V], F32, name=f"new{t}", align_bytes=64)
+            nc.scalar.activation(out=new[t][:], in_=diff[:], func=ACT.Silu, bias=zero[:])
 
         def put(t):
-            nc.vector.tensor_copy(out=y[t][:].indirect(dst_t[:]), in_=e[t][:])
-            for c, w in enumerate(PIECES):
-                cols = slice(starts[c], starts[c] + w)
-                if t == order[-1] and starts[c] < HALF:
-                    nc.vector.tensor_scalar(z_bf[c][:, :, t], y[t][:, cols], gt_t[:, t : t + 1], None, ALU.mult)
+            nc.vector.tensor_copy(out=y[t][:].indirect(dst_t[:]), in_=new[t][:])
+            weight = gt_t[:, t : t + 1]
+            for c, cols in enumerate(PIECES):
+                if t == ORDER[-1] and cols.stop <= HALF:
+                    nc.vector.tensor_scalar(z_bf[c][:, :, t], y[t][:, cols], weight, None, ALU.mult)
                 else:
-                    nc.scalar.activation(out=z_bf[c][:, :, t], in_=y[t][:, cols], func=ACT.Copy, scale=gt_t[:, t : t + 1])
+                    nc.scalar.activation(out=z_bf[c][:, :, t], in_=y[t][:, cols], func=ACT.Copy, scale=weight)
 
         deal_words(nc, w1w_dealt, w1w_raw)
-        fetch_dst(order[0])
-        fetch_dst(order[1])
-        fetch_src(order[0])
-        fetch_src(order[1])
-        fetch_dst(order[2])
-        put(order[0])
-        fetch_src(order[2])
-        fetch_dst(order[3])
-        put(order[1])
-        fetch_src(order[3])
-        put(order[2])
-        put(order[3])
+        for t in ORDER[:2]:
+            fetch_old(t)
+        for t in ORDER[:2]:
+            make_new(t)
+        for ahead, t in zip(ORDER[2:], ORDER[:2]):
+            fetch_old(ahead)
+            put(t)
+            make_new(ahead)
+        for t in ORDER[2:]:
+            put(t)
 
         out_rows = out_0.rearrange("(p t) j -> p t j", t=PACK)
         out_words = out_1[0].rearrange("p c r -> p (c r)").bitcast(I32)
-        o_codes = sb.tile([P, H], U32, name="o_codes", align_bytes=64)
-        o_scales = sb.tile([P, H], U8, name="o_scales", align_bytes=64)
-        free_banks = [f"bank{k}" for k in range(5)]
+        out_codes = sb.tile([P, H], U32, name="out_codes", align_bytes=64)
+        out_scales = sb.tile([P, H], U8, name="out_scales", align_bytes=64)
+        z_codes = sb.tile([P, H], U32, name="z_codes", align_bytes=64)
+        z_scales = sb.tile([P, H], U8, name="z_scales", align_bytes=64)
+        for c, cols in enumerate(PIECES):
+            quantize(nc, z_codes[:, cols], z_scales[:, cols], z_bf[c])
+
         banks = {}
-        for c, w in enumerate(PIECES):
-            z_codes = sb.tile([P, w], U32, name=f"z_codes{c}", align_bytes=64)
-            z_scales = sb.tile([P, w], U8, name=f"z_scales{c}", align_bytes=64)
-            nc.vector.quantize_mx(out=z_codes[:].bitcast(FP8X4), scales=z_scales[:], in_=z_bf[c][:].rearrange("p c t -> p (c t)"))
-            for t0, t1 in GROUPS[c]:
-                acc = ps.tile([P, t1 - t0, w], F32, name=f"acc{c}_{t0}", tag=free_banks.pop())
-                for t in range(t0, t1):
-                    nc.tensor.matmul_mx(
-                        out=acc[:, t - t0, :],
-                        lhsT=w1w_dealt[:, t, :].bitcast(FP8X4),
-                        lhsT_scale=w1s_dealt[:, t, :],
-                        rhs=z_codes[:].bitcast(FP8X4),
-                        rhs_scale=z_scales[:],
-                        start=True,
-                        stop=True,
-                    )
-                banks[(c, t0)] = acc
-        stored = 0
-        for c, w in enumerate(PIECES):
-            cols = slice(starts[c], starts[c] + w)
-            res = sb.tile([P, PACK, w], F32, name=f"res{c}", align_bytes=64)
-            res_bf = sb.tile([P, w, PACK], BF16, name=f"res_bf{c}", align_bytes=64)
-            for t0, t1 in GROUPS[c]:
-                nc.scalar.copy(out=res[:, t0:t1, :], in_=banks[(c, t0)][:])
-                if t1 % 2 == 0:
-                    rows = slice(t0 - t0 % 2, t1)
-                    nc.sync.dma_start(out=out_rows[:, rows, cols], in_=res[:, rows, :])
-            split = VEC_SHARE if cols.stop == H else w
-            o, i = weave(res_bf[:, 0:split, :], res[:, :, 0:split])
-            nc.vector.tensor_copy(out=o, in_=i)
-            if split < w:
-                o, i = weave(res_bf[:, split:w, :], res[:, :, split:w])
-                nc.scalar.copy(out=o, in_=i)
-            nc.vector.quantize_mx(out=o_codes[:, cols].bitcast(FP8X4), scales=o_scales[:, cols], in_=res_bf[:].rearrange("p c t -> p (c t)"))
-            if c >= len(PIECES) - 2:
-                run = slice(stored, cols.stop)
-                (nc.scalar if cols.stop == H else nc.sync).dma_start(out=out_words[:, run], in_=o_codes[:, run].bitcast(I32))
-                stored = cols.stop
-        for q in range(4):
-            queue = nc.scalar if q == 3 else nc.sync
-            queue.dma_start(out=out_2[0][4 * q : 4 * q + 4, :].bitcast(I32), in_=o_scales[32 * q : 32 * q + 4, :].bitcast(I32))
+        for h, half in enumerate(halves):
+            for t in range(PACK):
+                acc = ps.tile([P, 1, HALF], F32, name=f"acc{h}_{t}", tag=f"bank{PACK * h + t}")
+                for cols in PIECES[:2] if (h, t) == (0, 0) else [half]:
+                    into = acc[:, 0, cols.start - half.start : cols.stop - half.start]
+                    product(nc, into, w1w_dealt[:, t, :], w1s_dealt[:, t, :], z_codes[:, cols], z_scales[:, cols])
+                banks[(h, t)] = acc
+
+        for h, cols in enumerate(halves):
+            res = sb.tile([P, PACK, HALF], F32, name=f"res{h}", align_bytes=64)
+            res_bf = sb.tile([P, HALF, PACK], BF16, name=f"res_bf{h}", align_bytes=64)
+            for t in range(PACK):
+                copy = nc.vector.tensor_copy if (h, t) == (0, 2) else nc.scalar.copy
+                copy(out=res[:, t : t + 1, :], in_=banks[(h, t)][:])
+                for tiles in STORES[h]:
+                    if tiles.stop == t + 1:
+                        nc.sync.dma_start(out=out_rows[:, tiles, cols], in_=res[:, tiles, :])
+            interleave(nc, res_bf[:], res[:], [HALF, VEC_SHARE][h])
+            quantize(nc, out_codes[:, cols], out_scales[:, cols], res_bf)
+            [nc.sync, nc.scalar][h].dma_start(out=out_words[:, cols], in_=out_codes[:, cols].bitcast(I32))
+
+        for q in range(QUADS):
+            queue = nc.scalar if q == QUADS - 1 else nc.sync
+            queue.dma_start(
+                out=out_2[0][4 * q : 4 * q + 4, :].bitcast(I32),
+                in_=out_scales[32 * q : 32 * q + 4, :].bitcast(I32),
+            )

from contextlib import ExitStack

import concourse.mybir as mybir

F32 = mybir.dt.float32
BF16 = mybir.dt.bfloat16
I32 = mybir.dt.int32
U32 = mybir.dt.uint32
U16 = mybir.dt.uint16
U8 = mybir.dt.uint8
FP8X4 = mybir.dt.float8_e4m3fn_x4
ACT = mybir.ActivationFunctionType
ALU = mybir.AluOpType

K, T, S, V, N, H = 512, 2048, 512, 256, 512, 512
P = 128
PACK = 4
QUADS = 4
HALF = H // 2
PIECES = [slice(0, P), slice(P, HALF), slice(HALF, H)]
STORES = [[slice(0, 1), slice(1, 2), slice(2, 4)], [slice(0, 2), slice(2, 4)]]
VEC_SHARE = 160
ORDER = [2, 0, 1, 3]
FLOPS = 2 * K * S * H + 2 * S * N * H


def deal_words(nc, out, in_):
    nc.vector.tensor_copy(
        out=out[:].rearrange("p t (c i) -> p c t i", i=4),
        in_=in_[:].rearrange("p (c i t) -> p c t i", i=4, t=PACK),
    )


def deal_bytes(nc, out, in_):
    nc.vector.tensor_copy(out=out[:], in_=in_[:].rearrange("p (m t) -> p t m", t=PACK))


def place_scale_rows(queue, plane):
    rows = plane[:].rearrange("p t m -> p (t m)").bitcast(I32)
    for q in range(QUADS):
        queue.dma_start(out=rows[32 * q : 32 * q + 4, :], in_=rows[16 + 4 * q : 20 + 4 * q, :])


def interleave(nc, out, in_, vec_cols):
    width = out.shape[1]
    for copy, cols in ((nc.vector.tensor_copy, slice(0, vec_cols)), (nc.scalar.copy, slice(vec_cols, width))):
        if cols.start < cols.stop:
            copy(
                out=out[:, cols, :].rearrange("p (c i) t -> p c t i", i=4),
                in_=in_[:, :, cols].rearrange("p t (c i) -> p c t i", i=4),
            )


def quantize(nc, codes, scales, grouped):
    nc.vector.quantize_mx(out=codes.bitcast(FP8X4), scales=scales, in_=grouped[:].rearrange("p c t -> p (c t)"))


def product(nc, out, lhs_words, lhs_scales, rhs_codes, rhs_scales):
    nc.tensor.matmul_mx(
        out=out,
        lhsT=lhs_words.bitcast(FP8X4),
        lhsT_scale=lhs_scales,
        rhs=rhs_codes.bitcast(FP8X4),
        rhs_scale=rhs_scales,
        start=True,
        stop=True,
    )


def tile_picked_featput_silu_po_kernel(
    tc, x_words, x_scales, wa, gt, w1_words, w1_scales, offs, src, dst, out_0, out_1, out_2
):
    nc = tc.nc
    halves = [slice(0, HALF), slice(HALF, H)]
    with ExitStack() as ctx:
        lists = ctx.enter_context(tc.tile_pool(name="lists", bufs=1))
        sb = ctx.enter_context(tc.tile_pool(name="sb", bufs=1))
        ps = ctx.enter_context(tc.psum_pool(name="ps", bufs=1))

        offs_t = lists.tile([P, S // 16], U16, name="offs_t")
        src_t = lists.tile([P, V // 16], U16, name="src_t")
        dst_t = lists.tile([P, V // 16], U16, name="dst_t")

        zero_in = sb.tile([P, 1], F32, name="zero_in")
        zero = sb.tile([P, 1], F32, name="zero")
        nc.vector.memset(zero_in[:], 0.0)
        nc.scalar.activation(out=zero[:], in_=zero_in[:], func=ACT.Silu)

        xs_win = sb.tile([P, T], U8, name="xs_win", align_bytes=64)
        w1s_raw = sb.tile([P, N], U8, name="w1s_raw", align_bytes=64)
        for plane in (xs_win, w1s_raw):
            for lo, hi in ((0, 16), (32, 64), (64, P)):
                nc.vector.memset(plane[lo:hi, :].bitcast(I32), 0)

        xw_win = sb.tile([P, T], U32, name="xw_win", align_bytes=64)
        wa_raw = sb.tile([P, PACK, H], F32, name="wa_raw", align_bytes=64)
        gt_t = sb.tile([P, PACK], F32, name="gt_t", align_bytes=64)
        nc.sync.dma_start(offs_t[:], offs)
        nc.scalar.dma_start(out=w1s_raw[16:32, :].bitcast(I32), in_=w1_scales[0].bitcast(I32))
        nc.scalar.dma_start(out=gt_t[:], in_=gt.rearrange("(p t) o -> p (t o)", t=PACK))
        nc.sync.dma_start(out=xs_win[16:32, :].bitcast(I32), in_=x_scales[0].bitcast(I32))
        nc.sync.dma_start(out=xw_win[:].bitcast(I32), in_=x_words[0].rearrange("p c r -> p (c r)").bitcast(I32))
        nc.sync.dma_start(out=wa_raw[:], in_=wa.rearrange("(p j) c -> p j c", j=PACK))
        nc.sync.dma_start(src_t[:], src)
        nc.sync.dma_start(dst_t[:], dst)

        xs_got = sb.tile([P, S], U8, name="xs_got", align_bytes=64)
        xs_dealt = sb.tile([P, PACK, P], U8, name="xs_dealt", align_bytes=64)
        nc.vector.tensor_copy(out=xs_got[:], in_=xs_win[:].indirect(offs_t[:]))
        deal_bytes(nc, xs_dealt, xs_got)
        place_scale_rows(nc.scalar, xs_dealt)

        w1w_raw = sb.tile([P, N], U32, name="w1w_raw", tag="xs_got", align_bytes=64)
        nc.sync.dma_start(out=w1w_raw[:].bitcast(I32), in_=w1_words[0].rearrange("p c r -> p (c r)").bitcast(I32))
        w1s_dealt = sb.tile([P, PACK, P], U8, name="w1s_dealt", tag="xs_win", align_bytes=64)
        deal_bytes(nc, w1s_dealt, w1s_raw)
        place_scale_rows(nc.sync, w1s_dealt)

        xw_dealt = sb.tile([P, PACK, P], U32, name="xw_dealt", align_bytes=64)
        xw_got = sb.tile([P, S], U32, name="xw_got", align_bytes=64)
        nc.vector.tensor_copy(out=xw_got[:], in_=xw_win[:].indirect(offs_t[:]))
        deal_words(nc, xw_dealt, xw_got)

        wa_codes = sb.tile([P, H], U32, name="wa_codes", tag="xw_got", align_bytes=64)
        wa_scales = sb.tile([P, H], U8, name="wa_scales", align_bytes=64)
        wa_bf = [sb.tile([P, HALF, PACK], BF16, name=f"wa_bf{h}", align_bytes=64) for h in range(2)]
        for h, cols in enumerate(halves):
            interleave(nc, wa_bf[h][:], wa_raw[:, :, cols], VEC_SHARE)
        for h, cols in enumerate(halves):
            quantize(nc, wa_codes[:, cols], wa_scales[:, cols], wa_bf[h])

        y = [sb.tile([P, H], F32, name=f"y{t}", align_bytes=64) for t in range(PACK)]
        parts = [(t, cols) for cols in halves for t in ORDER[:2]] + [(t, slice(0, H)) for t in ORDER[2:]]
        for bank, (t, cols) in enumerate(parts):
            part = ps.tile([P, cols.stop - cols.start], F32, name=f"part{bank}", tag=f"bank{bank}")
            product(nc, part[:], xw_dealt[:, t, :], xs_dealt[:, t, :], wa_codes[:, cols], wa_scales[:, cols])
            nc.scalar.copy(out=y[t][:, cols], in_=part[:])

        w1w_dealt = sb.tile([P, PACK, P], U32, name="w1w_dealt", tag="wa_bf1", align_bytes=64)
        z_bf = [
            sb.tile([P, cols.stop - cols.start, PACK], BF16, name=f"z_bf{c}", align_bytes=64)
            for c, cols in enumerate(PIECES)
        ]
        old = {}
        new = {}

        def fetch_old(t):
            tag = f"new{ORDER[0]}" if t == ORDER[-1] else f"old{t}"
            old[t] = sb.tile([P, V], F32, name=f"old{t}", tag=tag, align_bytes=64)
            nc.vector.tensor_copy(out=old[t][:], in_=y[t][:].indirect(dst_t[:]))

        def make_new(t):
            diff = sb.tile([P, V], F32, name=f"diff{t}", tag=f"diff{ORDER.index(t) % 2}", align_bytes=64)
            nc.vector.tensor_tensor(diff[:], y[t][:].indirect(src_t[:]), old[t][:], ALU.subtract)
            new[t] = sb.tile([P, V], F32, name=f"new{t}", align_bytes=64)
            nc.scalar.activation(out=new[t][:], in_=diff[:], func=ACT.Silu, bias=zero[:])

        def put(t):
            nc.vector.tensor_copy(out=y[t][:].indirect(dst_t[:]), in_=new[t][:])
            weight = gt_t[:, t : t + 1]
            for c, cols in enumerate(PIECES):
                if t == ORDER[-1] and cols.stop <= HALF:
                    nc.vector.tensor_scalar(z_bf[c][:, :, t], y[t][:, cols], weight, None, ALU.mult)
                else:
                    nc.scalar.activation(out=z_bf[c][:, :, t], in_=y[t][:, cols], func=ACT.Copy, scale=weight)

        deal_words(nc, w1w_dealt, w1w_raw)
        for t in ORDER[:2]:
            fetch_old(t)
        for t in ORDER[:2]:
            make_new(t)
        for ahead, t in zip(ORDER[2:], ORDER[:2]):
            fetch_old(ahead)
            put(t)
            make_new(ahead)
        for t in ORDER[2:]:
            put(t)

        out_rows = out_0.rearrange("(p t) j -> p t j", t=PACK)
        out_words = out_1[0].rearrange("p c r -> p (c r)").bitcast(I32)
        out_codes = sb.tile([P, H], U32, name="out_codes", align_bytes=64)
        out_scales = sb.tile([P, H], U8, name="out_scales", align_bytes=64)
        z_codes = sb.tile([P, H], U32, name="z_codes", align_bytes=64)
        z_scales = sb.tile([P, H], U8, name="z_scales", align_bytes=64)
        for c, cols in enumerate(PIECES):
            quantize(nc, z_codes[:, cols], z_scales[:, cols], z_bf[c])

        banks = {}
        for h, half in enumerate(halves):
            for t in range(PACK):
                acc = ps.tile([P, 1, HALF], F32, name=f"acc{h}_{t}", tag=f"bank{PACK * h + t}")
                for cols in PIECES[:2] if (h, t) == (0, 0) else [half]:
                    into = acc[:, 0, cols.start - half.start : cols.stop - half.start]
                    product(nc, into, w1w_dealt[:, t, :], w1s_dealt[:, t, :], z_codes[:, cols], z_scales[:, cols])
                banks[(h, t)] = acc

        for h, cols in enumerate(halves):
            res = sb.tile([P, PACK, HALF], F32, name=f"res{h}", align_bytes=64)
            res_bf = sb.tile([P, HALF, PACK], BF16, name=f"res_bf{h}", align_bytes=64)
            for t in range(PACK):
                copy = nc.vector.tensor_copy if (h, t) == (0, 2) else nc.scalar.copy
                copy(out=res[:, t : t + 1, :], in_=banks[(h, t)][:])
                for tiles in STORES[h]:
                    if tiles.stop == t + 1:
                        nc.sync.dma_start(out=out_rows[:, tiles, cols], in_=res[:, tiles, :])
            interleave(nc, res_bf[:], res[:], [HALF, VEC_SHARE][h])
            quantize(nc, out_codes[:, cols], out_scales[:, cols], res_bf)
            [nc.sync, nc.scalar][h].dma_start(out=out_words[:, cols], in_=out_codes[:, cols].bitcast(I32))

        for q in range(QUADS):
            queue = nc.scalar if q == QUADS - 1 else nc.sync
            queue.dma_start(
                out=out_2[0][4 * q : 4 * q + 4, :].bitcast(I32),
                in_=out_scales[32 * q : 32 * q + 4, :].bitcast(I32),
            )
